import numpy as np, ml_dtypes
CORES = [24,32,56,88,96,104,30,38,62,94,102,110]
N = 12
import mx_ref
NC, G = 128, 4
C = np.float32(0.000979)
A = np.float32(0.021)
BF = ml_dtypes.bfloat16
def cut(t, i, w=512):
    return t[:, w * i:w * i + w]
def tile(rs):
    return np.stack(rs, axis=2).reshape(128, -1).astype(BF)
def layer(w, X):
    out = []
    for i in range(G):
        for t in range(len(X)):
            p = mx_ref.matmul(mx_ref.quantize(cut(w, len(X) * i + t)), X[t])
            z = p if t == 0 else z + p
        out.append(z)
    return out
def silu(z):
    z = z.astype(np.float64); e = np.exp(-np.abs(z))
    return (z * np.where(z >= 0, 1, e) / (1 + e)).astype(np.float32)
def gate(U, V):
    return [(silu(u * A) * v) * C for u, v in zip(U, V)]
def setup_inputs(rng):
    def f(*shape):
        return mx_ref.flush((rng.standard_normal(shape, dtype=np.float32) * np.exp2(rng.integers(-2, 3, shape[:-1] + (1,)))).astype(BF))
    return {"x": f(N, 128, 4 * NC), "u": f(N, 128, G * 512), "v": f(N, 128, G * 512), "w2": f(N, 128, N * 512)}
def setup_inputs_blocks(rng):
    d = setup_inputs(rng)
    for k in ("v", "w2"): d[k] = mx_ref.spread(d[k], rng, 2)
    for k in ("x", "u"): d[k] = mx_ref.spread(d[k], rng, 1)
    return d
def setup_inputs_wide(rng):
    d = setup_inputs(rng)
    for k in ("v", "w2"): d[k] = mx_ref.flush((d[k].astype(np.float32) * np.exp2(rng.integers(-5, 6, (N, 1, 1))).astype(np.float32)).astype(BF))
    return d
def setup_inputs_zeros(rng):
    d = setup_inputs(rng); v = d["x"].reshape(N, 128, -1, 4).copy()
    v[np.broadcast_to((rng.random((N, 1, v.shape[2], 1)) < 0.33), v.shape)] = 0
    d["x"] = v.reshape(d["x"].shape)
    return d
def reference(x, u, v, w2, own=None):
    h = np.zeros((N, 128, 4 * NC), BF)
    for j in range(N):
        X = [mx_ref.quantize(x[j])]
        h[j] = tile(gate(layer(u[j], X), layer(v[j], X)))
    use = h if own is None else own["h"]
    H = [mx_ref.quantize(use[j]) for j in range(N)]
    y = np.zeros((N, 128, NC), np.float32)
    for r in range(N):
        for j in range(N):
            p = mx_ref.matmul(mx_ref.quantize(cut(w2[r], j)), H[j])
            y[r] = p if j == 0 else y[r] + p
    return {"h": h, "y": y}

@@ -1,0 +1,205 @@
+from concourse.bass import DstId, RemoteDMATransfer
+from concourse.mybir import dt, AluOpType, ActivationFunctionType
+
+N = 12
+NC = 128
+NH = 2
+FA = 0.021
+FC = 0.000979
+
+SCRATCH = {
+    "xb": ("sbuf", [128, 512], "bfloat16"),
+    "ub": ("sbuf", [128, 2048], "bfloat16"),
+    "vb": ("sbuf", [128, 2048], "bfloat16"),
+    "wb": ("sbuf", [128, 512 * N], "bfloat16"),
+    "hb": ("sbuf", [128, 512], "bfloat16"),
+    "xq": ("sbuf", [128, NC], "float8_e4m3fn_x4"), "xs": ("sbuf", [128, NC], "uint8"),
+    "uq": ("sbuf", [128, 4 * NC], "float8_e4m3fn_x4"), "us": ("sbuf", [128, 4 * NC], "uint8"),
+    "vq": ("sbuf", [128, 4 * NC], "float8_e4m3fn_x4"), "vs": ("sbuf", [128, 4 * NC], "uint8"),
+    "wq": ("sbuf", [128, N * NC], "float8_e4m3fn_x4"), "ws": ("sbuf", [128, N * NC], "uint8"),
+    "hq": ("sbuf", [128, N * NC], "float8_e4m3fn_x4"), "hs": ("sbuf", [128, N * NC], "uint8"),
+    "sb": ("sbuf", [128, 512], "float32"),
+    "tb": ("sbuf", [128, 512], "float32"),
+    "yb": ("sbuf", [128, NC], "float32"),
+    "pu": ("psum", [128, 2048], "float32"),
+    "pv": ("psum", [128, 2048], "float32"),
+}
+SEMAPHORES = ["lx", "lu", "lv", "lw0", "lw1", "qx", "qu", "qv", "qw", "mu", "mv", "si", "tt", "sc", "hd", "ym", "yc",
+              "st", "sent"] + ["a%d" % j for j in range(N)]
+
+
+def _bits(m):
+    return [e for e in range(16) if (m >> e) & 1]
+
+
+def _plan(cores, topo):
+    chips = sorted({topo.chip(c) for c in cores})
+    every = range(topo.CHIPS * topo.CORES_PER_CHIP)
+    tile = {c: i for i, c in enumerate(cores)}
+    steps, arr, when = {}, {}, {}
+
+    def post(src, t0, tiles, groups, unit):
+        steps.setdefault(src, []).append((t0, tiles, groups))
+        for eng, dsts in groups:
+            for k, d in enumerate(dsts):
+                est = t0 + (k + 1) * unit * len(tiles)
+                arr.setdefault(d, {})[tiles[0]] = (tiles, 2 * len(eng), est)
+                for j in tiles:
+                    when[(d, j)] = est
+
+    def sibs(c):
+        return [r for r in cores if topo.chip(r) == topo.chip(c) and r != c]
+
+    relay = []
+    for c in cores:
+        A, d, j = topo.chip(c), topo.die(c), tile[c]
+        peers = [r for r in cores if topo.die(r) == d and topo.chip(r) != A]
+        peers.sort(key=lambda r: (chips.index(topo.chip(r)) - chips.index(A)) % len(chips))
+        direct = [r for r in peers if topo.may_write(c, r)]
+        rest = [r for r in peers if not topo.may_write(c, r)]
+        cand = [k for k in every if topo.chip(k) == A and topo.die(k) == d and k not in cores
+                and all(topo.may_write(k, r) for r in rest)]
+        helpers = cand[:min(NH, len(rest))]
+        off = _bits(topo.mask(c, direct[0]))
+        on = [e for e in _bits(topo.mask(c, sibs(c)[0])) if e not in off]
+        post(c, 0.0, [j], [(off, direct), (on, helpers + sibs(c))], 1.0)
+        for i, k in enumerate(helpers):
+            relay.append((k, j, rest[i::len(helpers)]))
+    for k, j, dsts in relay:
+        post(k, when[(k, j)] + 2.5, [j], [(_bits(topo.mask(k, dsts[0])), dsts)], 1.0)
+
+    def key(c):
+        return lambda j: (0 if topo.may_write(cores[j], c) else 1, when[(c, j)], j)
+
+    got = {c: sorted([j for j in range(len(cores)) if topo.die(cores[j]) == topo.die(c)
+                      and topo.chip(cores[j]) != topo.chip(c)], key=key(c)) for c in cores}
+    lay = {}
+    for A in chips:
+        order = []
+        for c in cores:
+            if topo.chip(c) == A:
+                order += [tile[c]] + got[c]
+        lay[A] = {j: p for p, j in enumerate(order)}
+    for c in cores:
+        for late in (0, 1):
+            run = [j for j in got[c] if key(c)(j)[0] == late]
+            if run:
+                post(c, max(when[(c, j)] for j in run) + 1.0, run, [(_bits(topo.mask(c, sibs(c)[0])), sibs(c))], 0.3)
+    return steps, arr, lay
+
+
+def rank_program(g, core, T, topo):
+    steps, arr, lay = _plan(T.cores, topo)
+    if core not in steps:
+        return
+    S = T.sem
+    me = T.rank_of(core)
+    sent = [0]
+
+    def view(buf, c, tiles, codes):
+        L = lay[topo.chip(c)]
+        p = L[tiles[0]]
+        assert [L[j] for j in tiles] == list(range(p, p + len(tiles)))
+        v = buf[:, NC * p:NC * (p + len(tiles))]
+        return v.bitcast(dt.uint8) if codes else v
+
+    def send(tiles, groups):
+        for buf, codes in ((T.hq, True), (T.hs, False)):
+            trs = []
+            for eng, dsts in groups:
+                ids = [topo.addr(d) for d in dsts]
+                trs.append(RemoteDMATransfer(
+                    dst_ids=[DstId(rid=a[0], pnc=a[1]) for a in ids], dma_engine_mask=sum(1 << e for e in eng),
+                    remote_sem=S["a%d" % tiles[0]], srcs=[view(buf, core, tiles, codes)],
+                    dsts=[view(buf, d, tiles, codes) for d in dsts]))
+                sent[0] += len(eng)
+            g.remote_dma_fused(trs, local_sem=S.sent)
+
+    for t0, tiles, groups in sorted(steps[core], key=lambda s: s[0]):
+        if tiles == [me]:
+            g.wait_ge(S.hd, 1)
+        else:
+            for j in tiles:
+                g.wait_ge(S["a%d" % j], arr[core][j][1])
+        send(tiles, groups)
+    g.wait_ge(S.sent, sent[0])
+    if me is None:
+        return
+
+    sy, sc, ve, te = g.sync, g.scalar, g.vector, g.tensor
+
+    def c(i, n=1):
+        return slice(NC * i, NC * (i + n))
+
+    def b(i):
+        return slice(512 * i, 512 * i + NC)
+
+    sy.dma_start(T.xb[:], T.x[:]).then_inc(S.lx, 16)
+    sc.dma_start(T.ub[:], T.u[:]).then_inc(S.lu, 16)
+    sy.dma_start(T.vb[:], T.v[:]).then_inc(S.lv, 16)
+    hN = N // 2
+    halves = [me // hN, 1 - me // hN]
+    for i, f in enumerate(halves):
+        sy.dma_start(T.wb[:, 512 * hN * f:512 * hN * (f + 1)], T.w2[:, 512 * hN * f:512 * hN * (f + 1)]).then_inc(S["lw%d" % i], 16)
+    sy.wait_ge(S.sc, 4)
+    sy.dma_start(T.h[:], T.hb[:]).then_inc(S.st, 16)
+
+    ve.wait_ge(S.lx, 16)
+    ve.quantize_mx(T.xq[:], T.xs[:], T.xb[:]).then_inc(S.qx, 1)
+    ve.wait_ge(S.lu, 16)
+    for i in range(4):
+        ve.quantize_mx(T.uq[:, c(i)], T.us[:, c(i)], T.ub[:, 512 * i:512 * i + 512]).then_inc(S.qu, 1)
+    ve.wait_ge(S.lv, 16)
+    for i in range(4):
+        ve.quantize_mx(T.vq[:, c(i)], T.vs[:, c(i)], T.vb[:, 512 * i:512 * i + 512]).then_inc(S.qv, 1)
+    for i in range(4):
+        ve.wait_ge(S.mv, i + 1)
+        ve.wait_ge(S.si, i + 1)
+        ve.tensor_tensor(T.tb[:, c(i)], T.sb[:, c(i)], T.pv[:, b(i)], AluOpType.mult).then_inc(S.tt, 1)
+    ve.wait_ge(S.tt, 4)
+    ve.tensor_scalar(T.hb[:, 3:512:4], T.tb[:, c(3)], FC, None, AluOpType.mult).then_inc(S.sc, 1)
+    ve.wait_ge(S.sc, 4)
+    own = lay[topo.chip(core)][me]
+    ve.quantize_mx(T.hq[:, c(own)], T.hs[:, c(own)], T.hb[:]).then_inc(S.hd, 1)
+    need = {}
+    for i, f in enumerate(halves):
+        ve.wait_ge(S["lw%d" % i], 16)
+        for k in range(2):
+            t = hN * f + 3 * k
+            ve.quantize_mx(T.wq[:, c(t, 3)], T.ws[:, c(t, 3)], T.wb[:, 512 * t:512 * (t + 3)]).then_inc(S.qw, 1)
+            for j in range(t, t + 3):
+                need[j] = 2 * i + k + 1
+    ve.wait_ge(S.ym, 1)
+    ve.tensor_copy(T.yb[:], T.pu[:, 0:NC]).then_inc(S.yc, 1)
+
+    for i in range(4):
+        sc.wait_ge(S.mu, i + 1)
+        sc.activation(T.sb[:, c(i)], T.pu[:, b(i)], ActivationFunctionType.Silu, scale=FA).then_inc(S.si, 1)
+    for i in range(3):
+        sc.wait_ge(S.tt, i + 1)
+        sc.activation(T.hb[:, i:512:4], T.tb[:, c(i)], ActivationFunctionType.Copy, scale=FC).then_inc(S.sc, 1)
+
+    te.wait_ge(S.qx, 1)
+    for i in range(4):
+        te.wait_ge(S.qu, i + 1)
+        te.matmul_mx(T.pu[:, b(i)], T.uq[:, c(i)], T.us[:, c(i)], T.xq[:], T.xs[:], True, True).then_inc(S.mu, 1)
+    for i in range(4):
+        te.wait_ge(S.qv, i + 1)
+        te.matmul_mx(T.pv[:, b(i)], T.vq[:, c(i)], T.vs[:, c(i)], T.xq[:], T.xs[:], True, True).then_inc(S.mv, 1)
+    te.wait_ge(S.si, 4)
+    te.wait_ge(S.hd, 1)
+    seq = [(me, None, 0)]
+    for tiles, cnt, est in sorted(arr[core].values(), key=lambda a: a[2]):
+        seq += [(j, tiles[0], cnt) for j in tiles]
+    L = lay[topo.chip(core)]
+    for n, (j, first, cnt) in enumerate(seq):
+        if first is not None:
+            te.wait_ge(S["a%d" % first], cnt)
+        te.wait_ge(S.qw, need[j])
+        mm = te.matmul_mx(T.pu[:, 0:NC], T.wq[:, c(j)], T.ws[:, c(j)], T.hq[:, c(L[j])], T.hs[:, c(L[j])],
+                          n == 0, n == N - 1)
+    mm.then_inc(S.ym, 1)
+
+    sy.wait_ge(S.yc, 1)
+    sy.dma_start(T.y[:], T.yb[:]).then_inc(S.st, 16)
+    sy.wait_ge(S.st, 32)

@@ -4,6 +4,7 @@ from concourse.mybir import dt, AluOpType, ActivationFunctionType
 N = 12
 NC = 128
 NH = 2
+FSPLIT = 4
 FA = 0.021
 FC = 0.000979
 
@@ -82,9 +83,12 @@ def _plan(cores, topo):
         lay[A] = {j: p for p, j in enumerate(order)}
     for c in cores:
         for late in (0, 1):
-            run = [j for j in got[c] if key(c)(j)[0] == late]
-            if run:
-                post(c, max(when[(c, j)] for j in run) + 1.0, run, [(_bits(topo.mask(c, sibs(c)[0])), sibs(c))], 0.3)
+            full = [j for j in got[c] if key(c)(j)[0] == late]
+            cut = (len(full) + 1) // 2 if len(full) >= FSPLIT else len(full)
+            for run in (full[:cut], full[cut:]):
+                if run:
+                    post(c, max(when[(c, j)] for j in run) + 1.0, run,
+                         [(_bits(topo.mask(c, sibs(c)[0])), sibs(c))], 0.3)
     return steps, arr, lay
 
 
@@ -104,7 +108,7 @@ def rank_program(g, core, T, topo):
         return v.bitcast(dt.uint8) if codes else v
 
     def send(tiles, groups):
-        for buf, codes in ((T.hq, True), (T.hs, False)):
+        for buf, codes in ((T.hq, True), (T.hs, False))[::-1 if len(tiles) == 1 else 1]:
             trs = []
             for eng, dsts in groups:
                 ids = [topo.addr(d) for d in dsts]
@@ -134,13 +138,17 @@ def rank_program(g, core, T, topo):
     def b(i):
         return slice(512 * i, 512 * i + NC)
 
+    blocks = [0, 1, 2, 3] if me < N // 2 else [3, 2, 1, 0]
+    blocks.sort(key=lambda k: k != me // 3)
+    need = {t: i + 1 for i, k in enumerate(blocks) for t in range(3 * k, 3 * k + 3)}
+    lo = 3 * min(blocks[:3])
+
     sy.dma_start(T.xb[:], T.x[:]).then_inc(S.lx, 16)
     sc.dma_start(T.ub[:], T.u[:]).then_inc(S.lu, 16)
     sy.dma_start(T.vb[:], T.v[:]).then_inc(S.lv, 16)
-    hN = N // 2
-    halves = [me // hN, 1 - me // hN]
-    for i, f in enumerate(halves):
-        sy.dma_start(T.wb[:, 512 * hN * f:512 * hN * (f + 1)], T.w2[:, 512 * hN * f:512 * hN * (f + 1)]).then_inc(S["lw%d" % i], 16)
+    sy.dma_start(T.wb[:, 512 * lo:512 * (lo + 9)], T.w2[:, 512 * lo:512 * (lo + 9)]).then_inc(S.lw0, 16)
+    k = blocks[3]
+    sy.dma_start(T.wb[:, 1536 * k:1536 * (k + 1)], T.w2[:, 1536 * k:1536 * (k + 1)]).then_inc(S.lw1, 16)
     sy.wait_ge(S.sc, 4)
     sy.dma_start(T.h[:], T.hb[:]).then_inc(S.st, 16)
 
@@ -161,14 +169,9 @@ def rank_program(g, core, T, topo):
     ve.wait_ge(S.sc, 4)
     own = lay[topo.chip(core)][me]
     ve.quantize_mx(T.hq[:, c(own)], T.hs[:, c(own)], T.hb[:]).then_inc(S.hd, 1)
-    need = {}
-    for i, f in enumerate(halves):
-        ve.wait_ge(S["lw%d" % i], 16)
-        for k in range(2):
-            t = hN * f + 3 * k
-            ve.quantize_mx(T.wq[:, c(t, 3)], T.ws[:, c(t, 3)], T.wb[:, 512 * t:512 * (t + 3)]).then_inc(S.qw, 1)
-            for j in range(t, t + 3):
-                need[j] = 2 * i + k + 1
+    for i, k in enumerate(blocks):
+        ve.wait_ge(S.lw0 if i < 3 else S.lw1, 16)
+        ve.quantize_mx(T.wq[:, c(3 * k, 3)], T.ws[:, c(3 * k, 3)], T.wb[:, 1536 * k:1536 * (k + 1)]).then_inc(S.qw, 1)
     ve.wait_ge(S.ym, 1)
     ve.tensor_copy(T.yb[:], T.pu[:, 0:NC]).then_inc(S.yc, 1)
 
@@ -188,11 +191,12 @@ def rank_program(g, core, T, topo):
         te.matmul_mx(T.pv[:, b(i)], T.vq[:, c(i)], T.vs[:, c(i)], T.xq[:], T.xs[:], True, True).then_inc(S.mv, 1)
     te.wait_ge(S.si, 4)
     te.wait_ge(S.hd, 1)
-    seq = [(me, None, 0)]
-    for tiles, cnt, est in sorted(arr[core].values(), key=lambda a: a[2]):
-        seq += [(j, tiles[0], cnt) for j in tiles]
+    seq = [(-1.0, me, None, 0)]
+    for tiles, cnt, est in arr[core].values():
+        seq += [(max(est, 7.0 if need[j] == 4 else 0.0), j, tiles[0], cnt) for j in tiles]
+    seq.sort(key=lambda a: a[0])
     L = lay[topo.chip(core)]
-    for n, (j, first, cnt) in enumerate(seq):
+    for n, (est, j, first, cnt) in enumerate(seq):
         if first is not None:
             te.wait_ge(S["a%d" % first], cnt)
         te.wait_ge(S.qw, need[j])

@@ -3,7 +3,7 @@ from concourse.mybir import dt, AluOpType, ActivationFunctionType
 
 N = 12
 NC = 128
-NH = 2
+ND = 3
 FSPLIT = 4
 FA = 0.021
 FC = 0.000979
@@ -25,8 +25,8 @@ SCRATCH = {
     "pu": ("psum", [128, 2048], "float32"),
     "pv": ("psum", [128, 2048], "float32"),
 }
-SEMAPHORES = ["lx", "lu", "lv", "lw0", "lw1", "qx", "qu", "qv", "qw", "mu", "mv", "si", "tt", "sc", "hd", "ym", "yc",
-              "st", "sent"] + ["a%d" % j for j in range(N)]
+SEMAPHORES = ["lx", "lu0", "lu1", "lv0", "lv1", "lw0", "lw1", "qx", "qu", "qv", "qw", "mu", "mv", "si", "tt", "sc", "hd",
+              "ym", "yc", "st", "sent"] + ["a%d" % j for j in range(N)] + ["p%d" % j for j in range(N)]
 
 
 def _bits(m):
@@ -37,14 +37,14 @@ def _plan(cores, topo):
     chips = sorted({topo.chip(c) for c in cores})
     every = range(topo.CHIPS * topo.CORES_PER_CHIP)
     tile = {c: i for i, c in enumerate(cores)}
-    steps, arr, when = {}, {}, {}
+    steps, arr, when, via = {}, {}, {}, {}
 
     def post(src, t0, tiles, groups, unit):
         steps.setdefault(src, []).append((t0, tiles, groups))
         for eng, dsts in groups:
             for k, d in enumerate(dsts):
                 est = t0 + (k + 1) * unit * len(tiles)
-                arr.setdefault(d, {})[tiles[0]] = (tiles, 2 * len(eng), est)
+                arr.setdefault(d, {})[tiles[0]] = (tiles, len(eng), est)
                 for j in tiles:
                     when[(d, j)] = est
 
@@ -56,21 +56,31 @@ def _plan(cores, topo):
         A, d, j = topo.chip(c), topo.die(c), tile[c]
         peers = [r for r in cores if topo.die(r) == d and topo.chip(r) != A]
         peers.sort(key=lambda r: (chips.index(topo.chip(r)) - chips.index(A)) % len(chips))
+        idle = [k for k in every if topo.chip(k) == A and topo.die(k) == d and k not in cores]
+        idle.sort(key=lambda k: sum(1 for r in peers if topo.may_write(k, r)))
         direct = [r for r in peers if topo.may_write(c, r)]
-        rest = [r for r in peers if not topo.may_write(c, r)]
-        cand = [k for k in every if topo.chip(k) == A and topo.die(k) == d and k not in cores
-                and all(topo.may_write(k, r) for r in rest)]
-        helpers = cand[:min(NH, len(rest))]
+        jobs = {}
+        for r in peers:
+            if r not in direct:
+                k = min([k for k in idle if topo.may_write(k, r)], key=lambda k: len(jobs.get(k, [])))
+                jobs.setdefault(k, []).append(r)
+        for r in direct[::-1]:
+            free = [k for k in idle if k not in jobs and topo.may_write(k, r)]
+            if len(direct) > ND and free:
+                jobs[free[0]] = [r]
+                direct.remove(r)
         off = _bits(topo.mask(c, direct[0]))
         on = [e for e in _bits(topo.mask(c, sibs(c)[0])) if e not in off]
-        post(c, 0.0, [j], [(off, direct), (on, helpers + sibs(c))], 1.0)
-        for i, k in enumerate(helpers):
-            relay.append((k, j, rest[i::len(helpers)]))
+        post(c, 0.0, [j], [(off, direct), (on, list(jobs) + sibs(c))], 1.0)
+        for k, dsts in jobs.items():
+            relay.append((k, j, dsts))
+            for r in dsts:
+                via[(r, j)] = 1
     for k, j, dsts in relay:
         post(k, when[(k, j)] + 2.5, [j], [(_bits(topo.mask(k, dsts[0])), dsts)], 1.0)
 
     def key(c):
-        return lambda j: (0 if topo.may_write(cores[j], c) else 1, when[(c, j)], j)
+        return lambda j: (via.get((c, j), 0), when[(c, j)], j)
 
     got = {c: sorted([j for j in range(len(cores)) if topo.die(cores[j]) == topo.die(c)
                       and topo.chip(cores[j]) != topo.chip(c)], key=key(c)) for c in cores}
@@ -107,25 +117,26 @@ def rank_program(g, core, T, topo):
         v = buf[:, NC * p:NC * (p + len(tiles))]
         return v.bitcast(dt.uint8) if codes else v
 
-    def send(tiles, groups):
-        for buf, codes in ((T.hq, True), (T.hs, False))[::-1 if len(tiles) == 1 else 1]:
-            trs = []
-            for eng, dsts in groups:
-                ids = [topo.addr(d) for d in dsts]
-                trs.append(RemoteDMATransfer(
-                    dst_ids=[DstId(rid=a[0], pnc=a[1]) for a in ids], dma_engine_mask=sum(1 << e for e in eng),
-                    remote_sem=S["a%d" % tiles[0]], srcs=[view(buf, core, tiles, codes)],
-                    dsts=[view(buf, d, tiles, codes) for d in dsts]))
-                sent[0] += len(eng)
-            g.remote_dma_fused(trs, local_sem=S.sent)
+    def send(tiles, groups, codes):
+        buf = T.hq if codes else T.hs
+        trs = []
+        for eng, dsts in groups:
+            ids = [topo.addr(d) for d in dsts]
+            trs.append(RemoteDMATransfer(
+                dst_ids=[DstId(rid=a[0], pnc=a[1]) for a in ids], dma_engine_mask=sum(1 << e for e in eng),
+                remote_sem=S[("a%d" if codes else "p%d") % tiles[0]], srcs=[view(buf, core, tiles, codes)],
+                dsts=[view(buf, d, tiles, codes) for d in dsts]))
+            sent[0] += len(eng)
+        g.remote_dma_fused(trs, local_sem=S.sent)
 
     for t0, tiles, groups in sorted(steps[core], key=lambda s: s[0]):
-        if tiles == [me]:
-            g.wait_ge(S.hd, 1)
-        else:
-            for j in tiles:
-                g.wait_ge(S["a%d" % j], arr[core][j][1])
-        send(tiles, groups)
+        for codes in (False, True):
+            if tiles == [me]:
+                g.wait_ge(S.hd, 1)
+            else:
+                for j in tiles:
+                    g.wait_ge(S[("a%d" if codes else "p%d") % j], arr[core][j][1])
+            send(tiles, groups, codes)
     g.wait_ge(S.sent, sent[0])
     if me is None:
         return
@@ -144,26 +155,38 @@ def rank_program(g, core, T, topo):
     lo = 3 * min(blocks[:3])
 
     sy.dma_start(T.xb[:], T.x[:]).then_inc(S.lx, 16)
-    sc.dma_start(T.ub[:], T.u[:]).then_inc(S.lu, 16)
-    sy.dma_start(T.vb[:], T.v[:]).then_inc(S.lv, 16)
+    sc.dma_start(T.ub[:, 0:512], T.u[:, 0:512]).then_inc(S.lu0, 16)
+    sy.dma_start(T.ub[:, 512:2048], T.u[:, 512:2048]).then_inc(S.lu1, 16)
+    sy.dma_start(T.vb[:, 0:1536], T.v[:, 0:1536]).then_inc(S.lv0, 16)
+    sy.dma_start(T.vb[:, 1536:2048], T.v[:, 1536:2048]).then_inc(S.lv1, 16)
     sy.dma_start(T.wb[:, 512 * lo:512 * (lo + 9)], T.w2[:, 512 * lo:512 * (lo + 9)]).then_inc(S.lw0, 16)
     k = blocks[3]
     sy.dma_start(T.wb[:, 1536 * k:1536 * (k + 1)], T.w2[:, 1536 * k:1536 * (k + 1)]).then_inc(S.lw1, 16)
     sy.wait_ge(S.sc, 4)
     sy.dma_start(T.h[:], T.hb[:]).then_inc(S.st, 16)
 
-    ve.wait_ge(S.lx, 16)
-    ve.quantize_mx(T.xq[:], T.xs[:], T.xb[:]).then_inc(S.qx, 1)
-    ve.wait_ge(S.lu, 16)
-    for i in range(4):
-        ve.quantize_mx(T.uq[:, c(i)], T.us[:, c(i)], T.ub[:, 512 * i:512 * i + 512]).then_inc(S.qu, 1)
-    ve.wait_ge(S.lv, 16)
-    for i in range(4):
+    def qv(i):
         ve.quantize_mx(T.vq[:, c(i)], T.vs[:, c(i)], T.vb[:, 512 * i:512 * i + 512]).then_inc(S.qv, 1)
-    for i in range(4):
+
+    def tt(i):
         ve.wait_ge(S.mv, i + 1)
         ve.wait_ge(S.si, i + 1)
         ve.tensor_tensor(T.tb[:, c(i)], T.sb[:, c(i)], T.pv[:, b(i)], AluOpType.mult).then_inc(S.tt, 1)
+
+    ve.wait_ge(S.lx, 16)
+    ve.quantize_mx(T.xq[:], T.xs[:], T.xb[:]).then_inc(S.qx, 1)
+    for i in range(4):
+        ve.wait_ge(S.lu0 if i == 0 else S.lu1, 16)
+        ve.quantize_mx(T.uq[:, c(i)], T.us[:, c(i)], T.ub[:, 512 * i:512 * i + 512]).then_inc(S.qu, 1)
+    ve.wait_ge(S.lv0, 16)
+    for i in range(3):
+        qv(i)
+    tt(0)
+    tt(1)
+    ve.wait_ge(S.lv1, 16)
+    qv(3)
+    tt(2)
+    tt(3)
     ve.wait_ge(S.tt, 4)
     ve.tensor_scalar(T.hb[:, 3:512:4], T.tb[:, c(3)], FC, None, AluOpType.mult).then_inc(S.sc, 1)
     ve.wait_ge(S.sc, 4)
@@ -198,6 +221,7 @@ def rank_program(g, core, T, topo):
     L = lay[topo.chip(core)]
     for n, (est, j, first, cnt) in enumerate(seq):
         if first is not None:
+            te.wait_ge(S["p%d" % first], cnt)
             te.wait_ge(S["a%d" % first], cnt)
         te.wait_ge(S.qw, need[j])
         mm = te.matmul_mx(T.pu[:, 0:NC], T.wq[:, c(j)], T.ws[:, c(j)], T.hq[:, c(L[j])], T.hs[:, c(L[j])],

from concourse.bass import DstId, RemoteDMATransfer
from concourse.mybir import dt, AluOpType, ActivationFunctionType

N = 12
NC = 128
ND = 3
FSPLIT = 4
FA = 0.021
FC = 0.000979

SCRATCH = {
    "xb": ("sbuf", [128, 512], "bfloat16"),
    "ub": ("sbuf", [128, 2048], "bfloat16"),
    "vb": ("sbuf", [128, 2048], "bfloat16"),
    "wb": ("sbuf", [128, 512 * N], "bfloat16"),
    "hb": ("sbuf", [128, 512], "bfloat16"),
    "xq": ("sbuf", [128, NC], "float8_e4m3fn_x4"), "xs": ("sbuf", [128, NC], "uint8"),
    "uq": ("sbuf", [128, 4 * NC], "float8_e4m3fn_x4"), "us": ("sbuf", [128, 4 * NC], "uint8"),
    "vq": ("sbuf", [128, 4 * NC], "float8_e4m3fn_x4"), "vs": ("sbuf", [128, 4 * NC], "uint8"),
    "wq": ("sbuf", [128, N * NC], "float8_e4m3fn_x4"), "ws": ("sbuf", [128, N * NC], "uint8"),
    "hq": ("sbuf", [128, N * NC], "float8_e4m3fn_x4"), "hs": ("sbuf", [128, N * NC], "uint8"),
    "sb": ("sbuf", [128, 512], "float32"),
    "tb": ("sbuf", [128, 512], "float32"),
    "yb": ("sbuf", [128, NC], "float32"),
    "pu": ("psum", [128, 2048], "float32"),
    "pv": ("psum", [128, 2048], "float32"),
}
SEMAPHORES = ["lx", "lu0", "lu1", "lv0", "lv1", "lw0", "lw1", "qx", "qu", "qv", "qw", "mu", "mv", "si", "tt", "sc", "hd",
              "ym", "yc", "st", "sent"] + ["a%d" % j for j in range(N)] + ["p%d" % j for j in range(N)]


def _bits(m):
    return [e for e in range(16) if (m >> e) & 1]


def _plan(cores, topo):
    chips = sorted({topo.chip(c) for c in cores})
    every = range(topo.CHIPS * topo.CORES_PER_CHIP)
    tile = {c: i for i, c in enumerate(cores)}
    steps, arr, when, via = {}, {}, {}, {}

    def post(src, t0, tiles, groups, unit):
        steps.setdefault(src, []).append((t0, tiles, groups))
        for eng, dsts in groups:
            for k, d in enumerate(dsts):
                est = t0 + (k + 1) * unit * len(tiles)
                arr.setdefault(d, {})[tiles[0]] = (tiles, len(eng), est)
                for j in tiles:
                    when[(d, j)] = est

    def sibs(c):
        return [r for r in cores if topo.chip(r) == topo.chip(c) and r != c]

    relay = []
    for c in cores:
        A, d, j = topo.chip(c), topo.die(c), tile[c]
        peers = [r for r in cores if topo.die(r) == d and topo.chip(r) != A]
        peers.sort(key=lambda r: (chips.index(topo.chip(r)) - chips.index(A)) % len(chips))
        idle = [k for k in every if topo.chip(k) == A and topo.die(k) == d and k not in cores]
        idle.sort(key=lambda k: sum(1 for r in peers if topo.may_write(k, r)))
        direct = [r for r in peers if topo.may_write(c, r)]
        jobs = {}
        for r in peers:
            if r not in direct:
                k = min([k for k in idle if topo.may_write(k, r)], key=lambda k: len(jobs.get(k, [])))
                jobs.setdefault(k, []).append(r)
        for r in direct[::-1]:
            free = [k for k in idle if k not in jobs and topo.may_write(k, r)]
            if len(direct) > ND and free:
                jobs[free[0]] = [r]
                direct.remove(r)
        off = _bits(topo.mask(c, direct[0]))
        on = [e for e in _bits(topo.mask(c, sibs(c)[0])) if e not in off]
        post(c, 0.0, [j], [(off, direct), (on, list(jobs) + sibs(c))], 1.0)
        for k, dsts in jobs.items():
            relay.append((k, j, dsts))
            for r in dsts:
                via[(r, j)] = 1
    for k, j, dsts in relay:
        post(k, when[(k, j)] + 2.5, [j], [(_bits(topo.mask(k, dsts[0])), dsts)], 1.0)

    def key(c):
        return lambda j: (via.get((c, j), 0), when[(c, j)], j)

    got = {c: sorted([j for j in range(len(cores)) if topo.die(cores[j]) == topo.die(c)
                      and topo.chip(cores[j]) != topo.chip(c)], key=key(c)) for c in cores}
    lay = {}
    for A in chips:
        order = []
        for c in cores:
            if topo.chip(c) == A:
                order += [tile[c]] + got[c]
        lay[A] = {j: p for p, j in enumerate(order)}
    for c in cores:
        for late in (0, 1):
            full = [j for j in got[c] if key(c)(j)[0] == late]
            cut = (len(full) + 1) // 2 if len(full) >= FSPLIT else len(full)
            for run in (full[:cut], full[cut:]):
                if run:
                    post(c, max(when[(c, j)] for j in run) + 1.0, run,
                         [(_bits(topo.mask(c, sibs(c)[0])), sibs(c))], 0.3)
    return steps, arr, lay


def rank_program(g, core, T, topo):
    steps, arr, lay = _plan(T.cores, topo)
    if core not in steps:
        return
    S = T.sem
    me = T.rank_of(core)
    sent = [0]

    def view(buf, c, tiles, codes):
        L = lay[topo.chip(c)]
        p = L[tiles[0]]
        assert [L[j] for j in tiles] == list(range(p, p + len(tiles)))
        v = buf[:, NC * p:NC * (p + len(tiles))]
        return v.bitcast(dt.uint8) if codes else v

    def send(tiles, groups, codes):
        buf = T.hq if codes else T.hs
        trs = []
        for eng, dsts in groups:
            ids = [topo.addr(d) for d in dsts]
            trs.append(RemoteDMATransfer(
                dst_ids=[DstId(rid=a[0], pnc=a[1]) for a in ids], dma_engine_mask=sum(1 << e for e in eng),
                remote_sem=S[("a%d" if codes else "p%d") % tiles[0]], srcs=[view(buf, core, tiles, codes)],
                dsts=[view(buf, d, tiles, codes) for d in dsts]))
            sent[0] += len(eng)
        g.remote_dma_fused(trs, local_sem=S.sent)

    for t0, tiles, groups in sorted(steps[core], key=lambda s: s[0]):
        for codes in (False, True):
            if tiles == [me]:
                g.wait_ge(S.hd, 1)
            else:
                for j in tiles:
                    g.wait_ge(S[("a%d" if codes else "p%d") % j], arr[core][j][1])
            send(tiles, groups, codes)
    g.wait_ge(S.sent, sent[0])
    if me is None:
        return

    sy, sc, ve, te = g.sync, g.scalar, g.vector, g.tensor

    def c(i, n=1):
        return slice(NC * i, NC * (i + n))

    def b(i):
        return slice(512 * i, 512 * i + NC)

    blocks = [0, 1, 2, 3] if me < N // 2 else [3, 2, 1, 0]
    blocks.sort(key=lambda k: k != me // 3)
    need = {t: i + 1 for i, k in enumerate(blocks) for t in range(3 * k, 3 * k + 3)}
    lo = 3 * min(blocks[:3])

    sy.dma_start(T.xb[:], T.x[:]).then_inc(S.lx, 16)
    sc.dma_start(T.ub[:, 0:512], T.u[:, 0:512]).then_inc(S.lu0, 16)
    sy.dma_start(T.ub[:, 512:2048], T.u[:, 512:2048]).then_inc(S.lu1, 16)
    sy.dma_start(T.vb[:, 0:1536], T.v[:, 0:1536]).then_inc(S.lv0, 16)
    sy.dma_start(T.vb[:, 1536:2048], T.v[:, 1536:2048]).then_inc(S.lv1, 16)
    sy.dma_start(T.wb[:, 512 * lo:512 * (lo + 9)], T.w2[:, 512 * lo:512 * (lo + 9)]).then_inc(S.lw0, 16)
    k = blocks[3]
    sy.dma_start(T.wb[:, 1536 * k:1536 * (k + 1)], T.w2[:, 1536 * k:1536 * (k + 1)]).then_inc(S.lw1, 16)
    sy.wait_ge(S.sc, 4)
    sy.dma_start(T.h[:], T.hb[:]).then_inc(S.st, 16)

    def qv(i):
        ve.quantize_mx(T.vq[:, c(i)], T.vs[:, c(i)], T.vb[:, 512 * i:512 * i + 512]).then_inc(S.qv, 1)

    def tt(i):
        ve.wait_ge(S.mv, i + 1)
        ve.wait_ge(S.si, i + 1)
        ve.tensor_tensor(T.tb[:, c(i)], T.sb[:, c(i)], T.pv[:, b(i)], AluOpType.mult).then_inc(S.tt, 1)

    ve.wait_ge(S.lx, 16)
    ve.quantize_mx(T.xq[:], T.xs[:], T.xb[:]).then_inc(S.qx, 1)
    for i in range(4):
        ve.wait_ge(S.lu0 if i == 0 else S.lu1, 16)
        ve.quantize_mx(T.uq[:, c(i)], T.us[:, c(i)], T.ub[:, 512 * i:512 * i + 512]).then_inc(S.qu, 1)
    ve.wait_ge(S.lv0, 16)
    for i in range(3):
        qv(i)
    tt(0)
    tt(1)
    ve.wait_ge(S.lv1, 16)
    qv(3)
    tt(2)
    tt(3)
    ve.wait_ge(S.tt, 4)
    ve.tensor_scalar(T.hb[:, 3:512:4], T.tb[:, c(3)], FC, None, AluOpType.mult).then_inc(S.sc, 1)
    ve.wait_ge(S.sc, 4)
    own = lay[topo.chip(core)][me]
    ve.quantize_mx(T.hq[:, c(own)], T.hs[:, c(own)], T.hb[:]).then_inc(S.hd, 1)
    for i, k in enumerate(blocks):
        ve.wait_ge(S.lw0 if i < 3 else S.lw1, 16)
        ve.quantize_mx(T.wq[:, c(3 * k, 3)], T.ws[:, c(3 * k, 3)], T.wb[:, 1536 * k:1536 * (k + 1)]).then_inc(S.qw, 1)
    ve.wait_ge(S.ym, 1)
    ve.tensor_copy(T.yb[:], T.pu[:, 0:NC]).then_inc(S.yc, 1)

    for i in range(4):
        sc.wait_ge(S.mu, i + 1)
        sc.activation(T.sb[:, c(i)], T.pu[:, b(i)], ActivationFunctionType.Silu, scale=FA).then_inc(S.si, 1)
    for i in range(3):
        sc.wait_ge(S.tt, i + 1)
        sc.activation(T.hb[:, i:512:4], T.tb[:, c(i)], ActivationFunctionType.Copy, scale=FC).then_inc(S.sc, 1)

    te.wait_ge(S.qx, 1)
    for i in range(4):
        te.wait_ge(S.qu, i + 1)
        te.matmul_mx(T.pu[:, b(i)], T.uq[:, c(i)], T.us[:, c(i)], T.xq[:], T.xs[:], True, True).then_inc(S.mu, 1)
    for i in range(4):
        te.wait_ge(S.qv, i + 1)
        te.matmul_mx(T.pv[:, b(i)], T.vq[:, c(i)], T.vs[:, c(i)], T.xq[:], T.xs[:], True, True).then_inc(S.mv, 1)
    te.wait_ge(S.si, 4)
    te.wait_ge(S.hd, 1)
    seq = [(-1.0, me, None, 0)]
    for tiles, cnt, est in arr[core].values():
        seq += [(max(est, 7.0 if need[j] == 4 else 0.0), j, tiles[0], cnt) for j in tiles]
    seq.sort(key=lambda a: a[0])
    L = lay[topo.chip(core)]
    for n, (est, j, first, cnt) in enumerate(seq):
        if first is not None:
            te.wait_ge(S["p%d" % first], cnt)
            te.wait_ge(S["a%d" % first], cnt)
        te.wait_ge(S.qw, need[j])
        mm = te.matmul_mx(T.pu[:, 0:NC], T.wq[:, c(j)], T.ws[:, c(j)], T.hq[:, c(L[j])], T.hs[:, c(L[j])],
                          n == 0, n == N - 1)
    mm.then_inc(S.ym, 1)

    sy.wait_ge(S.yc, 1)
    sy.dma_start(T.y[:], T.yb[:]).then_inc(S.st, 16)
    sy.wait_ge(S.st, 32)
